import numpy as np
import ml_dtypes


def mxq(x, axis, fmt="e4m3"):
    dtype, down = {"e4m3": (ml_dtypes.float8_e4m3fn, 7), "e5m2": (ml_dtypes.float8_e5m2, 14)}[fmt]
    v = np.moveaxis(np.asarray(x, np.float32).astype(ml_dtypes.bfloat16).astype(np.float64), axis, -1)
    blocks = v.reshape(v.shape[:-1] + (-1, 32))
    amax = np.abs(blocks).max(-1, keepdims=True)
    byte = np.maximum(np.where(amax > 0, np.frexp(amax)[1] - 1 + 127, 0) - down, 1)
    scale = np.exp2(byte - 127.0)
    codes = (blocks / scale).astype(np.float32).astype(dtype).astype(np.float64)
    return np.moveaxis((codes * scale).reshape(v.shape), -1, axis)


WIDE = False


def mx_kscale(k):
    if not WIDE:
        return np.ones(k)
    levels = np.array([10, -10, 5, -5, 0])
    if k % 512:
        return np.exp2(np.random.permutation(np.resize(levels, k // 32))).repeat(32)
    a = np.empty((k // 512, 16))
    for p in range(k // 512):
        a[p, :8] = np.random.permutation(np.resize(levels, 8))
        for g in range(8):
            far = levels[np.abs(levels - a[p, g]) >= 10]
            a[p, g + 8] = far[np.random.randint(len(far))]
    return np.exp2(a.ravel()).repeat(32)


def f64(x):
    return np.asarray(x).astype(np.float64)


def striped(idx):
    return np.tile(idx.reshape(-1, 16).T, (8, 1)).astype(np.uint16)


def unstriped(offs):
    return offs[:16].T.reshape(-1).astype(np.int64)


def relu2(v):
    return np.maximum(v, 0.0) ** 2


K, T, E, C, H, N = 512, 512, 8, 128, 512, 128


def by_expert(wq, xq):
    return np.concatenate([wq[e].T @ xq[:, e * C:(e + 1) * C] for e in range(E)], axis=1)


def setup_inputs():
    n = np.random.standard_normal
    s = mx_kscale(K)[:, None]
    u = mx_kscale(H)
    first = np.random.permutation(np.repeat(np.arange(E), T // E))
    second = (first + 1 + np.random.permutation(np.repeat(np.arange(E - 1), -(-T // (E - 1)))[:T])) % E
    while np.bincount(second, minlength=E).max() != T // E:
        load = np.bincount(second, minlength=E); hi, lo = int(load.argmax()), int(load.argmin())
        t = np.flatnonzero((second == hi) & (first != lo))[0]; second[t] = lo
    slot_token = np.empty(E * C, np.int64); pos = np.empty((2, T), np.int64); fill = np.zeros(E, np.int64)
    place = np.stack([np.random.permutation(C) for _ in range(E)])
    for r, deal in enumerate((first, second)):
        for t in np.random.permutation(T):
            e = deal[t]; j = e * C + place[e, fill[e]]; fill[e] += 1; slot_token[j] = t; pos[r, t] = j
    g = np.random.uniform(0.2, 0.8, T)
    return {
        "xT": (n((K, T)) * s).astype(np.float32),
        "w1": (n((E + 1, K, H)) / np.sqrt(K) / s[None] * u[None, None, :]).astype(np.float32),
        "w2": (n((E + 1, H, N)) / np.sqrt(H) / u[None, :, None] ** 2).astype(np.float32),
        "gate": np.stack([np.tile(g, (N, 1)), np.tile(1.0 - g, (N, 1))]).astype(np.float32),
        "offs": striped(slot_token),
        "pos1": striped(pos[0]),
        "pos2": striped(pos[1]),
    }


def reference(xT, w1, w2, gate, offs, pos1, pos2):
    idx = unstriped(offs)
    w1q, w2q = mxq(f64(w1), 1, "e4m3"), mxq(f64(w2), 1, "e4m3")
    xs = mxq(f64(xT), 0, "e4m3")
    hs = relu2(w1q[E].T @ xs)
    ys = w2q[E].T @ mxq(hs, 0, "e4m3")
    xq = mxq(f64(xT)[:, idx], 0, "e4m3")
    h = relu2(by_expert(w1q, xq))
    y = by_expert(w2q, mxq(h, 0, "e4m3"))
    return ys + f64(gate[0]) * y[:, unstriped(pos1)] + f64(gate[1]) * y[:, unstriped(pos2)]

@@ -1,0 +1,289 @@
+import concourse.mybir as mybir
+
+E, C, T, K, H, N = 8, 128, 512, 512, 512, 128
+P = 128
+FLOPS = 2 * K * H * (E * C + T) + 2 * H * N * (E * C + T)
+F32 = mybir.dt.float32
+BF16 = mybir.dt.bfloat16
+U32 = mybir.dt.uint32
+U16 = mybir.dt.uint16
+U8 = mybir.dt.uint8
+FP8X4 = mybir.dt.float8_e4m3fn_x4
+ACT = mybir.ActivationFunctionType
+ALU = mybir.AluOpType
+GROUP = 512
+
+
+def tile_moe_shr_mlp_relu2_kernel(tc, xT, w1, w2, gate, offs, pos1, pos2, out):
+    nc = tc.nc
+    with (
+        tc.tile_pool(name="keep", bufs=1) as keep,
+        tc.psum_pool(name="ps_a", bufs=5) as ps_a,
+        tc.psum_pool(name="ps_y", bufs=2) as ps_y,
+        tc.psum_pool(name="ps_s", bufs=1) as ps_s,
+    ):
+        offs_t = keep.tile([P, E * C // 16], U16, name="offs_t")
+        nc.sync.dma_start(offs_t[:], offs)
+        x_raw, raw, bf, qz, accs, sh, misc = [], {}, {}, {}, {}, {}, {}
+        xv = xT.rearrange("(p j) t -> p j t", j=4)
+        for u in range(2):
+            xr = keep.tile([P, 2, T], F32, name=f"x_raw{u}")
+            nc.sync.dma_start(xr[:], xv[:, 2 * u : 2 * u + 2, :])
+            x_raw.append(xr)
+
+        def load_w1(e):
+            t = keep.tile([P, 4, H], F32, name=f"w1_raw{e}")
+            nc.sync.dma_start(t[:], w1[e].rearrange("(p j) i -> p j i", j=4))
+            raw[f"w1_{e}"] = t
+
+        def load_w2(name, e0, n):
+            t = keep.tile([P, n, 4, N], F32, name=name + "_raw")
+            nc.sync.dma_start(t[:], w2[e0 : e0 + n].rearrange("e (p j) n -> p e j n", j=4))
+            raw[name] = t
+
+        def load_gates():
+            pos = []
+            for i, src in enumerate((pos1, pos2)):
+                t = keep.tile([P, T // 16], U16, name=f"pos{i}")
+                nc.sync.dma_start(t[:], src)
+                pos.append(t)
+            g = keep.tile([P, 2, T], F32, name="gates")
+            nc.sync.dma_start(g[:], gate.rearrange("r p t -> p r t"))
+            misc["g"], misc["pos"] = g, pos
+
+        load_w1(6)
+        load_w1(8)
+        load_w1(4)
+        load_w1(3)
+        load_gates()
+        load_w1(7)
+        load_w1(1)
+        load_w2("w2_A", 0, 4)
+        load_w1(5)
+        load_w2("w28", 8, 1)
+        load_w1(0)
+        load_w1(2)
+        load_w2("w2_B", 4, 4)
+
+        warm = keep.tile([P, 8], F32, name="warm")
+        nc.gpsimd.memset(warm[:], 0.0)
+        warm_out = keep.tile([P, 8], F32, name="warm_out")
+        nc.scalar.activation(warm_out[:], warm[:], ACT.Square)
+
+        def copy_on(engine, dst, src):
+            if engine == "V":
+                nc.vector.tensor_copy(dst, src)
+            else:
+                nc.scalar.copy(dst, src)
+
+        x_pair = keep.tile([P, 2, T, 2], BF16, name="x_pair", align_bytes=64)
+        XV = 320
+        for u in range(2):
+            src = x_raw[u][:].rearrange("p j t -> p t j")
+            nc.vector.tensor_copy(x_pair[:, u, 0:XV, :], src[:, 0:XV, :])
+            if XV < T:
+                nc.scalar.copy(x_pair[:, u, XV:T, :], src[:, XV:T, :])
+        words = x_pair[:].rearrange("p u t j -> p (u t j)").bitcast(U32)
+        gx = keep.tile([P, E * C, 2], U32, name="gx", align_bytes=64)
+        CUTS = (0, 384, 768, 1024)
+
+        def gath(g, u):
+            lo, hi = CUTS[g], CUTS[g + 1]
+            nc.vector.tensor_copy(gx[:, lo:hi, u], words[:, u * T : (u + 1) * T].indirect(offs_t[:, lo // 16 : hi // 16]))
+
+        def quant(in_, width, name):
+            codes = keep.tile([P, width], U32, name=name + "_q", align_bytes=64)
+            scales = keep.tile([P, width], U8, name=name + "_s", align_bytes=64)
+            nc.vector.quantize_mx(out=codes[:].bitcast(FP8X4), scales=scales[:], in_=in_)
+            return codes, scales
+
+        def qx(g):
+            qz[f"x{g}"] = quant(gx[:, g * GROUP : (g + 1) * GROUP, :].rearrange("p s u -> p (s u)").bitcast(BF16), GROUP, f"gx{g}")
+
+        def xall(engine):
+            t = keep.tile([P, T, 2, 2], BF16, name="x_all", align_bytes=64)
+            copy_on(engine, t[:], x_pair[:].rearrange("p u t j -> p t u j"))
+            bf["xs"] = t
+
+        def qxs():
+            qz["xs"] = quant(bf["xs"][:].rearrange("p t u j -> p (t u j)"), T, "xs")
+
+        def lay(name, parts):
+            n = 4 * raw[name].shape[-1] * (raw[name].shape[1] if raw[name].shape[-1] == N else 1)
+            d = keep.tile([P, n], BF16, name=name + "_bf", align_bytes=64)
+            if name.startswith("w1"):
+                dst = d[:].rearrange("p (t m j) -> p m j t", t=4, j=4)
+                src = raw[name][:].rearrange("p j (m t) -> p m j t", t=4)
+            else:
+                dst = d[:].rearrange("p (e n j) -> p e n j", n=N, j=4)
+                src = raw[name][:].rearrange("p e j n -> p e n j")
+            lo = 0
+            for engine, hi in parts:
+                if name == "w28" or name.startswith("w1"):
+                    if name == "w28":
+                        copy_on(engine, dst[:, 0, lo:hi], src[:, 0, lo:hi])
+                    else:
+                        copy_on(engine, dst[:, lo:hi], src[:, lo:hi])
+                else:
+                    copy_on(engine, dst[:, lo:hi], src[:, lo:hi])
+                lo = hi
+            bf[name] = d
+
+        def q(name):
+            qz[name] = quant(bf[name][:], bf[name].shape[1] // 4, name)
+
+        def mm_layer1(weights, tokens, c0):
+            acc = ps_a.tile([P, 4, C], F32, name="acc")
+            for t in range(4):
+                cols = slice(t * P, (t + 1) * P)
+                nc.tensor.matmul_mx(
+                    out=acc[:, t, :],
+                    lhsT=weights[0][:, cols].bitcast(FP8X4),
+                    lhsT_scale=weights[1][:, cols],
+                    rhs=tokens[0][:, c0 : c0 + C].bitcast(FP8X4),
+                    rhs_scale=tokens[1][:, c0 : c0 + C],
+                    start=True,
+                    stop=True,
+                )
+            return acc
+
+        def mm(e):
+            accs[e] = mm_layer1(qz[f"w1_{e}"], qz[f"x{e * C // GROUP}"], e * C % GROUP)
+
+        def mms(g):
+            accs[f"s{g}"] = mm_layer1(qz["w1_8"], qz["xs"], g * C)
+
+        def relu(e, r):
+            nc.scalar.activation(
+                r.rearrange("p (c t) -> p c t", t=4), accs[e][:].rearrange("p t c -> p c t"), ACT.Relu
+            )
+
+        def square(engine, h, r):
+            if engine == "V":
+                nc.vector.tensor_tensor(h, r, r, ALU.mult)
+            else:
+                nc.scalar.activation(h, r, ACT.Square)
+
+        def qh(codes, scales, h):
+            nc.vector.quantize_mx(out=codes.bitcast(FP8X4), scales=scales, in_=h)
+
+        def second(weights, c0, codes, scales, dst):
+            nc.tensor.matmul_mx(
+                out=dst,
+                lhsT=weights[0][:, c0 : c0 + N].bitcast(FP8X4),
+                lhsT_scale=weights[1][:, c0 : c0 + N],
+                rhs=codes.bitcast(FP8X4),
+                rhs_scale=scales,
+                start=True,
+                stop=True,
+            )
+
+        yt = keep.tile([P, E * C], F32, name="yt")
+        hs_q = keep.tile([P, T], U32, name="hs_q", align_bytes=64)
+        hs_s = keep.tile([P, T], U8, name="hs_s", align_bytes=64)
+        ys = ps_s.tile([P, T], F32, name="ys")
+        ot = keep.tile([P, T], F32, name="ot")
+
+        lay("w1_8", [("S", 128)])
+        xall("S")
+        lay("w1_0", [("S", 128)])
+        lay("w1_6", [("V", 64), ("S", 128)])
+        gath(0, 1)
+        lay("w1_3", [("V", 96), ("S", 128)])
+        lay("w2_A", [("V", 4)])
+        qxs()
+        q("w1_8")
+        gath(1, 1)
+        gath(2, 1)
+        gath(1, 0)
+        lay("w1_2", [("V", 96), ("S", 128)])
+        mms(1)
+        q("w1_3")
+        gath(0, 0)
+        lay("w1_1", [("S", 128)])
+        q("w1_2")
+        mms(0)
+        rs_0 = keep.tile([P, 1024], F32, name="rs_0")
+        relu("s1", rs_0[:, 512:1024])
+        gath(2, 0)
+        qx(0)
+        lay("w28", [("V", 64), ("S", 128)])
+        mm(2)
+        mm(3)
+        q("w1_1")
+        relu(2, raw["w1_1"][:].rearrange("p j i -> p (j i)")[:, 0:1024][:, 0:512])
+        q("w1_0")
+        mm(0)
+        relu("s0", rs_0[:, 0:512])
+        lay("w2_B", [("V", 3), ("S", 4)])
+        mm(1)
+        lay("w1_7", [("V", 64), ("S", 128)])
+        q("w1_6")
+        lay("w1_5", [("V", 128)])
+        qx(1)
+        q("w1_7")
+        q("w2_A")
+        mm(6)
+        relu(3, raw["w1_1"][:].rearrange("p j i -> p (j i)")[:, 0:1024][:, 512:1024])
+        mms(2)
+        relu(1, raw["w1_0"][:].rearrange("p j i -> p (j i)")[:, 0:1024][:, 512:1024])
+        mm(7)
+        relu(6, raw["w1_6"][:].rearrange("p j i -> p (j i)")[:, 0:1024][:, 0:512])
+        lay("w1_4", [("S", 128)])
+        relu(0, raw["w1_0"][:].rearrange("p j i -> p (j i)")[:, 0:1024][:, 0:512])
+        h_0 = keep.tile([P, 1024], BF16, name="h_0", align_bytes=64)
+        square("S", h_0[:], raw["w1_0"][:].rearrange("p j i -> p (j i)")[:, 0:1024])
+        rs_1 = keep.tile([P, 1024], F32, name="rs_1")
+        relu("s2", rs_1[:, 0:512])
+        q("w1_5")
+        relu(7, raw["w1_6"][:].rearrange("p j i -> p (j i)")[:, 0:1024][:, 512:1024])
+        q("w2_B")
+        q("w1_4")
+        square("S", bf["w1_4"][:, 0:1024], raw["w1_6"][:].rearrange("p j i -> p (j i)")[:, 0:1024])
+        qh(qz["w1_0"][0][:, 0:256], qz["w1_0"][1][:, 0:256], h_0[:])
+        mms(3)
+        mm(5)
+        mm(4)
+        square("V", bf["w1_4"][:, 1024:2048], raw["w1_1"][:].rearrange("p j i -> p (j i)")[:, 0:1024])
+        relu(4, raw["w1_1"][:].rearrange("p j i -> p (j i)")[:, 1024:2048][:, 0:512])
+        relu("s3", rs_1[:, 512:1024])
+        qh(qz["w1_0"][0][:, 256:512], qz["w1_0"][1][:, 256:512], bf["w1_4"][:, 0:1024])
+        relu(5, raw["w1_1"][:].rearrange("p j i -> p (j i)")[:, 1024:2048][:, 512:1024])
+        hh_1 = keep.tile([P, 1024], BF16, name="hh_1", align_bytes=64)
+        square("S", hh_1[:], rs_1[:])
+        yp_3 = ps_y.tile([P, 256], F32, name="yp")
+        second(qz["w2_B"], 256, qz["w1_0"][0][:, 256:512][:, 0:128], qz["w1_0"][1][:, 256:512][:, 0:128], yp_3[:, 0:128])
+        second(qz["w2_B"], 384, qz["w1_0"][0][:, 256:512][:, 128:256], qz["w1_0"][1][:, 256:512][:, 128:256], yp_3[:, 128:256])
+        square("V", bf["w1_3"][:, 0:1024], raw["w1_1"][:].rearrange("p j i -> p (j i)")[:, 1024:2048])
+        yp_0 = ps_y.tile([P, 256], F32, name="yp")
+        second(qz["w2_A"], 0, qz["w1_0"][0][:, 0:256][:, 0:128], qz["w1_0"][1][:, 0:256][:, 0:128], yp_0[:, 0:128])
+        second(qz["w2_A"], 128, qz["w1_0"][0][:, 0:256][:, 128:256], qz["w1_0"][1][:, 0:256][:, 128:256], yp_0[:, 128:256])
+        nc.scalar.copy(yt[:, 768:1024], yp_3[:])
+        hh_0 = keep.tile([P, 1024], BF16, name="hh_0", align_bytes=64)
+        square("V", hh_0[:], rs_0[:])
+        q("w28")
+        qh(qz["w1_7"][0][:, 0:256], qz["w1_7"][1][:, 0:256], bf["w1_3"][:, 0:1024])
+        yp_2 = ps_y.tile([P, 256], F32, name="yp")
+        second(qz["w2_B"], 0, qz["w1_7"][0][:, 0:256][:, 0:128], qz["w1_7"][1][:, 0:256][:, 0:128], yp_2[:, 0:128])
+        second(qz["w2_B"], 128, qz["w1_7"][0][:, 0:256][:, 128:256], qz["w1_7"][1][:, 0:256][:, 128:256], yp_2[:, 128:256])
+        qh(hs_q[:, 256:512], hs_s[:, 256:512], hh_1[:])
+        qh(hs_q[:, 0:256], hs_s[:, 0:256], hh_0[:])
+        qh(qz["w1_2"][0][:, 0:256], qz["w1_2"][1][:, 0:256], bf["w1_4"][:, 1024:2048])
+        yp_1 = ps_y.tile([P, 256], F32, name="yp")
+        second(qz["w2_A"], 256, qz["w1_2"][0][:, 0:256][:, 0:128], qz["w1_2"][1][:, 0:256][:, 0:128], yp_1[:, 0:128])
+        second(qz["w2_A"], 384, qz["w1_2"][0][:, 0:256][:, 128:256], qz["w1_2"][1][:, 0:256][:, 128:256], yp_1[:, 128:256])
+        nc.scalar.copy(yt[:, 256:512], yp_1[:])
+        nc.scalar.copy(yt[:, 512:768], yp_2[:])
+        second(qz["w28"], 0, hs_q[:, 256:512], hs_s[:, 256:512], ys[:, 256:512])
+        nc.scalar.copy(yt[:, 0:256], yp_0[:])
+        part_0 = keep.tile([P, T], F32, name="part_0")
+        nc.vector.tensor_tensor(part_0[:], yt[:].indirect(misc["pos"][0][:]), misc["g"][:, 0, :], ALU.mult)
+        part_1 = keep.tile([P, T], F32, name="part_1")
+        nc.vector.tensor_tensor(part_1[:], yt[:].indirect(misc["pos"][1][:]), misc["g"][:, 1, :], ALU.mult)
+        both = keep.tile([P, T], F32, name="both")
+        nc.vector.tensor_tensor(both[:], part_0[:], part_1[:], ALU.add)
+        second(qz["w28"], 0, hs_q[:, 0:256], hs_s[:, 0:256], ys[:, 0:256])
+        nc.vector.tensor_tensor(ot[:, 0:256], ys[:, 0:256], both[:, 0:256], ALU.add)
+        nc.sync.dma_start(out[:, 0:256], ot[:, 0:256])
+        nc.vector.tensor_tensor(ot[:, 256:512], ys[:, 256:512], both[:, 256:512], ALU.add)
+        nc.sync.dma_start(out[:, 256:512], ot[:, 256:512])

@@ -11,60 +11,47 @@ U8 = mybir.dt.uint8
 FP8X4 = mybir.dt.float8_e4m3fn_x4
 ACT = mybir.ActivationFunctionType
 ALU = mybir.AluOpType
-GROUP = 512
+CUTS = (0, 384, 768, 1024)
+W2 = {"w2_A": (0, 4), "w2_B": (4, 2), "w2_C": (6, 2), "w28": (8, 1)}
 
 
 def tile_moe_shr_mlp_relu2_kernel(tc, xT, w1, w2, gate, offs, pos1, pos2, out):
     nc = tc.nc
     with (
         tc.tile_pool(name="keep", bufs=1) as keep,
-        tc.psum_pool(name="ps_a", bufs=5) as ps_a,
-        tc.psum_pool(name="ps_y", bufs=2) as ps_y,
-        tc.psum_pool(name="ps_s", bufs=1) as ps_s,
+        tc.psum_pool(name="ps", bufs=1) as ps,
     ):
         offs_t = keep.tile([P, E * C // 16], U16, name="offs_t")
         nc.sync.dma_start(offs_t[:], offs)
-        x_raw, raw, bf, qz, accs, sh, misc = [], {}, {}, {}, {}, {}, {}
+        x_raw, raw, bf, qz, accs, misc, yp = [], {}, {}, {}, {}, {}, {}
         xv = xT.rearrange("(p j) t -> p j t", j=4)
         for u in range(2):
             xr = keep.tile([P, 2, T], F32, name=f"x_raw{u}")
             nc.sync.dma_start(xr[:], xv[:, 2 * u : 2 * u + 2, :])
             x_raw.append(xr)
 
-        def load_w1(e):
-            t = keep.tile([P, 4, H], F32, name=f"w1_raw{e}")
-            nc.sync.dma_start(t[:], w1[e].rearrange("(p j) i -> p j i", j=4))
-            raw[f"w1_{e}"] = t
+        def load(name):
+            if name == "g":
+                pos = []
+                for i, src in enumerate((pos1, pos2)):
+                    t = keep.tile([P, T // 16], U16, name=f"pos{i}")
+                    nc.sync.dma_start(t[:], src)
+                    pos.append(t)
+                g = keep.tile([P, 2, T], F32, name="gates")
+                nc.sync.dma_start(g[:], gate.rearrange("r p t -> p r t"))
+                misc["g"], misc["pos"] = g, pos
+            elif name in W2:
+                e0, n = W2[name]
+                t = keep.tile([P, n, 4, N], F32, name=name + "_raw")
+                nc.sync.dma_start(t[:], w2[e0 : e0 + n].rearrange("e (p j) n -> p e j n", j=4))
+                raw[name] = t
+            else:
+                t = keep.tile([P, 4, H], F32, name=name + "_raw")
+                nc.sync.dma_start(t[:], w1[int(name[3:])].rearrange("(p j) i -> p j i", j=4))
+                raw[name] = t
 
-        def load_w2(name, e0, n):
-            t = keep.tile([P, n, 4, N], F32, name=name + "_raw")
-            nc.sync.dma_start(t[:], w2[e0 : e0 + n].rearrange("e (p j) n -> p e j n", j=4))
-            raw[name] = t
-
-        def load_gates():
-            pos = []
-            for i, src in enumerate((pos1, pos2)):
-                t = keep.tile([P, T // 16], U16, name=f"pos{i}")
-                nc.sync.dma_start(t[:], src)
-                pos.append(t)
-            g = keep.tile([P, 2, T], F32, name="gates")
-            nc.sync.dma_start(g[:], gate.rearrange("r p t -> p r t"))
-            misc["g"], misc["pos"] = g, pos
-
-        load_w1(6)
-        load_w1(8)
-        load_w1(4)
-        load_w1(3)
-        load_gates()
-        load_w1(7)
-        load_w1(1)
-        load_w2("w2_A", 0, 4)
-        load_w1(5)
-        load_w2("w28", 8, 1)
-        load_w1(0)
-        load_w1(2)
-        load_w2("w2_B", 4, 4)
-
+        for name in ["w1_4","w1_3","w1_7","w1_6","w2_A","w1_8","w2_C","w1_5","w28","w1_0","w1_2","w1_1","w2_B","g"]:
+            load(name)
         warm = keep.tile([P, 8], F32, name="warm")
         nc.gpsimd.memset(warm[:], 0.0)
         warm_out = keep.tile([P, 8], F32, name="warm_out")
@@ -73,19 +60,22 @@ def tile_moe_shr_mlp_relu2_kernel(tc, xT, w1, w2, gate, offs, pos1, pos2, out):
         def copy_on(engine, dst, src):
             if engine == "V":
                 nc.vector.tensor_copy(dst, src)
-            else:
+            elif engine == "S":
                 nc.scalar.copy(dst, src)
+            else:
+                nc.gpsimd.tensor_scalar(dst, src, 1.0, 0.0, ALU.mult, ALU.add)
 
         x_pair = keep.tile([P, 2, T, 2], BF16, name="x_pair", align_bytes=64)
         XV = 320
-        for u in range(2):
+
+        def cast(u):
             src = x_raw[u][:].rearrange("p j t -> p t j")
             nc.vector.tensor_copy(x_pair[:, u, 0:XV, :], src[:, 0:XV, :])
             if XV < T:
                 nc.scalar.copy(x_pair[:, u, XV:T, :], src[:, XV:T, :])
+
         words = x_pair[:].rearrange("p u t j -> p (u t j)").bitcast(U32)
         gx = keep.tile([P, E * C, 2], U32, name="gx", align_bytes=64)
-        CUTS = (0, 384, 768, 1024)
 
         def gath(g, u):
             lo, hi = CUTS[g], CUTS[g + 1]
@@ -97,8 +87,8 @@ def tile_moe_shr_mlp_relu2_kernel(tc, xT, w1, w2, gate, offs, pos1, pos2, out):
             nc.vector.quantize_mx(out=codes[:].bitcast(FP8X4), scales=scales[:], in_=in_)
             return codes, scales
 
-        def qx(g):
-            qz[f"x{g}"] = quant(gx[:, g * GROUP : (g + 1) * GROUP, :].rearrange("p s u -> p (s u)").bitcast(BF16), GROUP, f"gx{g}")
+        def qx(h):
+            qz[f"x{h}"] = quant(gx[:, h * 512 : (h + 1) * 512, :].rearrange("p s u -> p (s u)").bitcast(BF16), 512, f"gx{h}")
 
         def xall(engine):
             t = keep.tile([P, T, 2, 2], BF16, name="x_all", align_bytes=64)
@@ -109,21 +99,18 @@ def tile_moe_shr_mlp_relu2_kernel(tc, xT, w1, w2, gate, offs, pos1, pos2, out):
             qz["xs"] = quant(bf["xs"][:].rearrange("p t u j -> p (t u j)"), T, "xs")
 
         def lay(name, parts):
-            n = 4 * raw[name].shape[-1] * (raw[name].shape[1] if raw[name].shape[-1] == N else 1)
-            d = keep.tile([P, n], BF16, name=name + "_bf", align_bytes=64)
-            if name.startswith("w1"):
-                dst = d[:].rearrange("p (t m j) -> p m j t", t=4, j=4)
-                src = raw[name][:].rearrange("p j (m t) -> p m j t", t=4)
-            else:
+            if name in W2:
+                d = keep.tile([P, W2[name][1] * 4 * N], BF16, name=name + "_bf", align_bytes=64)
                 dst = d[:].rearrange("p (e n j) -> p e n j", n=N, j=4)
                 src = raw[name][:].rearrange("p e j n -> p e n j")
+            else:
+                d = keep.tile([P, 4 * H], BF16, name=name + "_bf", align_bytes=64)
+                dst = d[:].rearrange("p (t m j) -> p m j t", t=4, j=4)
+                src = raw[name][:].rearrange("p j (m t) -> p m j t", t=4)
             lo = 0
             for engine, hi in parts:
-                if name == "w28" or name.startswith("w1"):
-                    if name == "w28":
-                        copy_on(engine, dst[:, 0, lo:hi], src[:, 0, lo:hi])
-                    else:
-                        copy_on(engine, dst[:, lo:hi], src[:, lo:hi])
+                if name in W2:
+                    copy_on(engine, dst[:, :, lo:hi, :], src[:, :, lo:hi, :])
                 else:
                     copy_on(engine, dst[:, lo:hi], src[:, lo:hi])
                 lo = hi
@@ -132,8 +119,8 @@ def tile_moe_shr_mlp_relu2_kernel(tc, xT, w1, w2, gate, offs, pos1, pos2, out):
         def q(name):
             qz[name] = quant(bf[name][:], bf[name].shape[1] // 4, name)
 
-        def mm_layer1(weights, tokens, c0):
-            acc = ps_a.tile([P, 4, C], F32, name="acc")
+        def layer1(key, weights, tokens, c0):
+            acc = ps.tile([P, 4, C], F32, name=f"acc{len(accs) % 5}")
             for t in range(4):
                 cols = slice(t * P, (t + 1) * P)
                 nc.tensor.matmul_mx(
@@ -145,18 +132,20 @@ def tile_moe_shr_mlp_relu2_kernel(tc, xT, w1, w2, gate, offs, pos1, pos2, out):
                     start=True,
                     stop=True,
                 )
-            return acc
+            accs[key] = acc
 
         def mm(e):
-            accs[e] = mm_layer1(qz[f"w1_{e}"], qz[f"x{e * C // GROUP}"], e * C % GROUP)
+            layer1(e, qz[f"w1_{e}"], qz[f"x{e // 4}"], e % 4 * C)
 
         def mms(g):
-            accs[f"s{g}"] = mm_layer1(qz["w1_8"], qz["xs"], g * C)
+            layer1(f"s{g}", qz["w1_8"], qz["xs"], g * C)
 
-        def relu(e, r):
-            nc.scalar.activation(
-                r.rearrange("p (c t) -> p c t", t=4), accs[e][:].rearrange("p t c -> p c t"), ACT.Relu
-            )
+        def relu(key, r, engine="S"):
+            dst, src = r.rearrange("p (c t) -> p c t", t=4), accs[key][:].rearrange("p t c -> p c t")
+            if engine == "V":
+                nc.vector.tensor_scalar_max(dst, src, 0.0)
+            else:
+                nc.scalar.activation(dst, src, ACT.Relu)
 
         def square(engine, h, r):
             if engine == "V":
@@ -167,7 +156,8 @@ def tile_moe_shr_mlp_relu2_kernel(tc, xT, w1, w2, gate, offs, pos1, pos2, out):
         def qh(codes, scales, h):
             nc.vector.quantize_mx(out=codes.bitcast(FP8X4), scales=scales, in_=h)
 
-        def second(weights, c0, codes, scales, dst):
+        def second(name, c0, codes, scales, dst):
+            weights = qz[name]
             nc.tensor.matmul_mx(
                 out=dst,
                 lhsT=weights[0][:, c0 : c0 + N].bitcast(FP8X4),
@@ -179,111 +169,121 @@ def tile_moe_shr_mlp_relu2_kernel(tc, xT, w1, w2, gate, offs, pos1, pos2, out):
             )
 
         yt = keep.tile([P, E * C], F32, name="yt")
-        hs_q = keep.tile([P, T], U32, name="hs_q", align_bytes=64)
-        hs_s = keep.tile([P, T], U8, name="hs_s", align_bytes=64)
-        ys = ps_s.tile([P, T], F32, name="ys")
+        ys = ps.tile([P, T], F32, name="ys")
         ot = keep.tile([P, T], F32, name="ot")
 
-        lay("w1_8", [("S", 128)])
-        xall("S")
-        lay("w1_0", [("S", 128)])
-        lay("w1_6", [("V", 64), ("S", 128)])
-        gath(0, 1)
-        lay("w1_3", [("V", 96), ("S", 128)])
-        lay("w2_A", [("V", 4)])
-        qxs()
-        q("w1_8")
-        gath(1, 1)
-        gath(2, 1)
-        gath(1, 0)
-        lay("w1_2", [("V", 96), ("S", 128)])
-        mms(1)
-        q("w1_3")
+        lay("w1_8", [("V", 96), ("S", 128)])
+        lay("w1_0", [("V", 128)])
+        lay("w1_3", [("V", 64), ("S", 128)])
+        lay("w1_7", [("S", 128)])
+        lay("w1_1", [("V", 96), ("S", 128)])
+        lay("w28", [("V", 80), ("S", 128)])
+        cast(1)
+        cast(0)
+        lay("w1_4", [("V", 48), ("S", 128)])
         gath(0, 0)
-        lay("w1_1", [("S", 128)])
-        q("w1_2")
-        mms(0)
-        rs_0 = keep.tile([P, 1024], F32, name="rs_0")
-        relu("s1", rs_0[:, 512:1024])
-        gath(2, 0)
-        qx(0)
-        lay("w28", [("V", 64), ("S", 128)])
-        mm(2)
-        mm(3)
-        q("w1_1")
-        relu(2, raw["w1_1"][:].rearrange("p j i -> p (j i)")[:, 0:1024][:, 0:512])
-        q("w1_0")
-        mm(0)
-        relu("s0", rs_0[:, 0:512])
-        lay("w2_B", [("V", 3), ("S", 4)])
-        mm(1)
-        lay("w1_7", [("V", 64), ("S", 128)])
-        q("w1_6")
-        lay("w1_5", [("V", 128)])
-        qx(1)
-        q("w1_7")
-        q("w2_A")
-        mm(6)
-        relu(3, raw["w1_1"][:].rearrange("p j i -> p (j i)")[:, 0:1024][:, 512:1024])
-        mms(2)
-        relu(1, raw["w1_0"][:].rearrange("p j i -> p (j i)")[:, 0:1024][:, 512:1024])
-        mm(7)
-        relu(6, raw["w1_6"][:].rearrange("p j i -> p (j i)")[:, 0:1024][:, 0:512])
-        lay("w1_4", [("S", 128)])
-        relu(0, raw["w1_0"][:].rearrange("p j i -> p (j i)")[:, 0:1024][:, 0:512])
-        h_0 = keep.tile([P, 1024], BF16, name="h_0", align_bytes=64)
-        square("S", h_0[:], raw["w1_0"][:].rearrange("p j i -> p (j i)")[:, 0:1024])
-        rs_1 = keep.tile([P, 1024], F32, name="rs_1")
-        relu("s2", rs_1[:, 0:512])
-        q("w1_5")
-        relu(7, raw["w1_6"][:].rearrange("p j i -> p (j i)")[:, 0:1024][:, 512:1024])
-        q("w2_B")
         q("w1_4")
-        square("S", bf["w1_4"][:, 0:1024], raw["w1_6"][:].rearrange("p j i -> p (j i)")[:, 0:1024])
-        qh(qz["w1_0"][0][:, 0:256], qz["w1_0"][1][:, 0:256], h_0[:])
-        mms(3)
+        gath(1, 0)
+        gath(1, 1)
+        q("w1_8")
+        q("w1_1")
+        gath(0, 1)
+        xall("S")
+        q("w1_7")
+        lay("w1_6", [("V", 48), ("S", 128)])
+        lay("w2_A", [("V", 64), ("S", 128)])
+        qx(0)
+        gath(2, 0)
+        lay("w2_B", [("V", 128)])
+        q("w2_B")
+        qxs()
+        lay("w1_2", [("V", 128)])
+        lay("w1_5", [("V", 80), ("S", 128)])
+        gath(2, 1)
+        q("w1_6")
+        q("w1_0")
+        q("w1_2")
+        mms(1)
+        qx(1)
+        q("w1_5")
+        mms(0)
         mm(5)
-        mm(4)
-        square("V", bf["w1_4"][:, 1024:2048], raw["w1_1"][:].rearrange("p j i -> p (j i)")[:, 0:1024])
-        relu(4, raw["w1_1"][:].rearrange("p j i -> p (j i)")[:, 1024:2048][:, 0:512])
-        relu("s3", rs_1[:, 512:1024])
-        qh(qz["w1_0"][0][:, 256:512], qz["w1_0"][1][:, 256:512], bf["w1_4"][:, 0:1024])
-        relu(5, raw["w1_1"][:].rearrange("p j i -> p (j i)")[:, 1024:2048][:, 512:1024])
-        hh_1 = keep.tile([P, 1024], BF16, name="hh_1", align_bytes=64)
-        square("S", hh_1[:], rs_1[:])
-        yp_3 = ps_y.tile([P, 256], F32, name="yp")
-        second(qz["w2_B"], 256, qz["w1_0"][0][:, 256:512][:, 0:128], qz["w1_0"][1][:, 256:512][:, 0:128], yp_3[:, 0:128])
-        second(qz["w2_B"], 384, qz["w1_0"][0][:, 256:512][:, 128:256], qz["w1_0"][1][:, 256:512][:, 128:256], yp_3[:, 128:256])
-        square("V", bf["w1_3"][:, 0:1024], raw["w1_1"][:].rearrange("p j i -> p (j i)")[:, 1024:2048])
-        yp_0 = ps_y.tile([P, 256], F32, name="yp")
-        second(qz["w2_A"], 0, qz["w1_0"][0][:, 0:256][:, 0:128], qz["w1_0"][1][:, 0:256][:, 0:128], yp_0[:, 0:128])
-        second(qz["w2_A"], 128, qz["w1_0"][0][:, 0:256][:, 128:256], qz["w1_0"][1][:, 0:256][:, 128:256], yp_0[:, 128:256])
-        nc.scalar.copy(yt[:, 768:1024], yp_3[:])
-        hh_0 = keep.tile([P, 1024], BF16, name="hh_0", align_bytes=64)
-        square("V", hh_0[:], rs_0[:])
+        relu("s1", raw["w1_0"][:].rearrange("p j i -> p (j i)")[:, 0:1024][:, 512:1024])
+        mm(0)
+        q("w1_3")
+        mm(3)
         q("w28")
-        qh(qz["w1_7"][0][:, 0:256], qz["w1_7"][1][:, 0:256], bf["w1_3"][:, 0:1024])
-        yp_2 = ps_y.tile([P, 256], F32, name="yp")
-        second(qz["w2_B"], 0, qz["w1_7"][0][:, 0:256][:, 0:128], qz["w1_7"][1][:, 0:256][:, 0:128], yp_2[:, 0:128])
-        second(qz["w2_B"], 128, qz["w1_7"][0][:, 0:256][:, 128:256], qz["w1_7"][1][:, 0:256][:, 128:256], yp_2[:, 128:256])
-        qh(hs_q[:, 256:512], hs_s[:, 256:512], hh_1[:])
-        qh(hs_q[:, 0:256], hs_s[:, 0:256], hh_0[:])
-        qh(qz["w1_2"][0][:, 0:256], qz["w1_2"][1][:, 0:256], bf["w1_4"][:, 1024:2048])
-        yp_1 = ps_y.tile([P, 256], F32, name="yp")
-        second(qz["w2_A"], 256, qz["w1_2"][0][:, 0:256][:, 0:128], qz["w1_2"][1][:, 0:256][:, 0:128], yp_1[:, 0:128])
-        second(qz["w2_A"], 384, qz["w1_2"][0][:, 0:256][:, 128:256], qz["w1_2"][1][:, 0:256][:, 128:256], yp_1[:, 128:256])
-        nc.scalar.copy(yt[:, 256:512], yp_1[:])
-        nc.scalar.copy(yt[:, 512:768], yp_2[:])
-        second(qz["w28"], 0, hs_q[:, 256:512], hs_s[:, 256:512], ys[:, 256:512])
-        nc.scalar.copy(yt[:, 0:256], yp_0[:])
+        relu("s0", raw["w1_0"][:].rearrange("p j i -> p (j i)")[:, 0:1024][:, 0:512])
+        mm(6)
+        mm(4)
+        r_3 = keep.tile([P, 1024], F32, name="r_3", align_bytes=64)
+        relu(6, r_3[:][:, 0:512])
+        relu(3, raw["w1_5"][:].rearrange("p j i -> p (j i)")[:, 0:1024][:, 512:1024])
+        relu(5, raw["w1_7"][:].rearrange("p j i -> p (j i)")[:, 0:1024][:, 512:1024])
+        relu(4, raw["w1_7"][:].rearrange("p j i -> p (j i)")[:, 0:1024][:, 0:512])
+        square("V", raw["w1_2"][:].rearrange("p j i -> p (j i)")[:, 0:512].bitcast(BF16), raw["w1_0"][:].rearrange("p j i -> p (j i)")[:, 0:1024])
+        mm(1)
+        relu(0, raw["w1_0"][:].rearrange("p j i -> p (j i)")[:, 1024:2048][:, 0:512])
+        mm(2)
+        mm(7)
+        relu(7, r_3[:][:, 512:1024])
+        mms(2)
+        square("S", raw["w1_1"][:].rearrange("p j i -> p (j i)")[:, 0:512].bitcast(BF16), raw["w1_7"][:].rearrange("p j i -> p (j i)")[:, 0:1024])
+        relu(1, raw["w1_0"][:].rearrange("p j i -> p (j i)")[:, 1024:2048][:, 512:1024])
+        lay("w2_C", [("S", 128)])
+        square("V", raw["w1_7"][:].rearrange("p j i -> p (j i)")[:, 1024:1536].bitcast(BF16), r_3[:])
+        relu("s2", raw["w1_5"][:].rearrange("p j i -> p (j i)")[:, 1024:2048][:, 0:512])
+        relu(2, raw["w1_5"][:].rearrange("p j i -> p (j i)")[:, 0:1024][:, 0:512])
+        square("S", raw["w1_1"][:].rearrange("p j i -> p (j i)")[:, 512:1024].bitcast(BF16), raw["w1_5"][:].rearrange("p j i -> p (j i)")[:, 0:1024])
+        hq_3 = keep.tile([P, 256], U32, name="hq_3", align_bytes=64)
+        hz_3 = keep.tile([P, 256], U8, name="hz_3", align_bytes=64)
+        qh(hq_3[:], hz_3[:], raw["w1_7"][:].rearrange("p j i -> p (j i)")[:, 1024:1536].bitcast(BF16))
+        mms(3)
+        hq_1 = keep.tile([P, 256], U32, name="hq_1", align_bytes=64)
+        hz_1 = keep.tile([P, 256], U8, name="hz_1", align_bytes=64)
+        qh(hq_1[:], hz_1[:], raw["w1_1"][:].rearrange("p j i -> p (j i)")[:, 512:1024].bitcast(BF16))
+        q("w2_C")
+        yp[3] = ps.tile([P, 256], F32, name="yp0")
+        second("w2_C", 0, hq_3[:, 0:128], hz_3[:, 0:128], yp[3][:, 0:128])
+        second("w2_C", 128, hq_3[:, 128:256], hz_3[:, 128:256], yp[3][:, 128:256])
+        q("w2_A")
+        hq_2 = keep.tile([P, 256], U32, name="hq_2", align_bytes=64)
+        hz_2 = keep.tile([P, 256], U8, name="hz_2", align_bytes=64)
+        qh(hq_2[:], hz_2[:], raw["w1_1"][:].rearrange("p j i -> p (j i)")[:, 0:512].bitcast(BF16))
+        square("S", raw["w1_6"][:].rearrange("p j i -> p (j i)")[:, 0:512].bitcast(BF16), raw["w1_0"][:].rearrange("p j i -> p (j i)")[:, 1024:2048])
+        relu("s3", raw["w1_5"][:].rearrange("p j i -> p (j i)")[:, 1024:2048][:, 512:1024])
+        hq_0 = keep.tile([P, 256], U32, name="hq_0", align_bytes=64)
+        hz_0 = keep.tile([P, 256], U8, name="hz_0", align_bytes=64)
+        qh(hq_0[:], hz_0[:], raw["w1_6"][:].rearrange("p j i -> p (j i)")[:, 0:512].bitcast(BF16))
+        yp[1] = ps.tile([P, 256], F32, name="yp1")
+        second("w2_A", 256, hq_1[:, 0:128], hz_1[:, 0:128], yp[1][:, 0:128])
+        second("w2_A", 384, hq_1[:, 128:256], hz_1[:, 128:256], yp[1][:, 128:256])
+        nc.scalar.copy(yt[:, 768:1024], yp[3][:])
+        yp[2] = ps.tile([P, 256], F32, name="yp0")
+        second("w2_B", 0, hq_2[:, 0:128], hz_2[:, 0:128], yp[2][:, 0:128])
+        second("w2_B", 128, hq_2[:, 128:256], hz_2[:, 128:256], yp[2][:, 128:256])
+        nc.scalar.copy(yt[:, 256:512], yp[1][:])
+        nc.scalar.copy(yt[:, 512:768], yp[2][:])
+        yp[0] = ps.tile([P, 256], F32, name="yp1")
+        second("w2_A", 0, hq_0[:, 0:128], hz_0[:, 0:128], yp[0][:, 0:128])
+        second("w2_A", 128, hq_0[:, 128:256], hz_0[:, 128:256], yp[0][:, 128:256])
+        nc.scalar.copy(yt[:, 0:256], yp[0][:])
+        square("V", raw["w1_7"][:].rearrange("p j i -> p (j i)")[:, 1536:2048].bitcast(BF16), raw["w1_5"][:].rearrange("p j i -> p (j i)")[:, 1024:2048])
         part_0 = keep.tile([P, T], F32, name="part_0")
         nc.vector.tensor_tensor(part_0[:], yt[:].indirect(misc["pos"][0][:]), misc["g"][:, 0, :], ALU.mult)
         part_1 = keep.tile([P, T], F32, name="part_1")
         nc.vector.tensor_tensor(part_1[:], yt[:].indirect(misc["pos"][1][:]), misc["g"][:, 1, :], ALU.mult)
+        hq_s1 = keep.tile([P, 256], U32, name="hq_s1", align_bytes=64)
+        hz_s1 = keep.tile([P, 256], U8, name="hz_s1", align_bytes=64)
+        qh(hq_s1[:], hz_s1[:], raw["w1_7"][:].rearrange("p j i -> p (j i)")[:, 1536:2048].bitcast(BF16))
+        hq_s0 = keep.tile([P, 256], U32, name="hq_s0", align_bytes=64)
+        hz_s0 = keep.tile([P, 256], U8, name="hz_s0", align_bytes=64)
+        qh(hq_s0[:], hz_s0[:], raw["w1_2"][:].rearrange("p j i -> p (j i)")[:, 0:512].bitcast(BF16))
+        second("w28", 0, hq_s0[:], hz_s0[:], ys[:, 0:256])
+        second("w28", 0, hq_s1[:], hz_s1[:], ys[:, 256:512])
         both = keep.tile([P, T], F32, name="both")
         nc.vector.tensor_tensor(both[:], part_0[:], part_1[:], ALU.add)
-        second(qz["w28"], 0, hs_q[:, 0:256], hs_s[:, 0:256], ys[:, 0:256])
-        nc.vector.tensor_tensor(ot[:, 0:256], ys[:, 0:256], both[:, 0:256], ALU.add)
-        nc.sync.dma_start(out[:, 0:256], ot[:, 0:256])
         nc.vector.tensor_tensor(ot[:, 256:512], ys[:, 256:512], both[:, 256:512], ALU.add)
         nc.sync.dma_start(out[:, 256:512], ot[:, 256:512])
+        nc.vector.tensor_tensor(ot[:, 0:256], ys[:, 0:256], both[:, 0:256], ALU.add)
+        nc.sync.dma_start(out[:, 0:256], ot[:, 0:256])

@@ -12,7 +12,8 @@ FP8X4 = mybir.dt.float8_e4m3fn_x4
 ACT = mybir.ActivationFunctionType
 ALU = mybir.AluOpType
 CUTS = (0, 384, 768, 1024)
-W2 = {"w2_A": (0, 4), "w2_B": (4, 2), "w2_C": (6, 2), "w28": (8, 1)}
+GROUPS = {}
+W2 = {"w2_A": (0, 4), "w2_B": (4, 4), "w28": (8, 1)}
 
 
 def tile_moe_shr_mlp_relu2_kernel(tc, xT, w1, w2, gate, offs, pos1, pos2, out):
@@ -23,15 +24,21 @@ def tile_moe_shr_mlp_relu2_kernel(tc, xT, w1, w2, gate, offs, pos1, pos2, out):
     ):
         offs_t = keep.tile([P, E * C // 16], U16, name="offs_t")
         nc.sync.dma_start(offs_t[:], offs)
+        bf_all = {}
         x_raw, raw, bf, qz, accs, misc, yp = [], {}, {}, {}, {}, {}, {}
         xv = xT.rearrange("(p j) t -> p j t", j=4)
         for u in range(2):
             xr = keep.tile([P, 2, T], F32, name=f"x_raw{u}")
-            nc.sync.dma_start(xr[:], xv[:, 2 * u : 2 * u + 2, :])
+            (nc.sync if u else nc.scalar).dma_start(xr[:], xv[:, 2 * u : 2 * u + 2, :])
             x_raw.append(xr)
 
         def load(name):
-            if name == "g":
+            if isinstance(name, tuple):
+                a, b = sorted(int(k[3:]) for k in name)
+                t = keep.tile([P, 2, 4, H], F32, name=f"w1_raw{a}_{b}")
+                nc.sync.dma_start(t[:], w1[a : b + 1 : b - a].rearrange("e (p j) i -> p e j i", j=4))
+                raw[f"w1_{a}"], raw[f"w1_{b}"] = t[:, 0], t[:, 1]
+            elif name == "g":
                 pos = []
                 for i, src in enumerate((pos1, pos2)):
                     t = keep.tile([P, T // 16], U16, name=f"pos{i}")
@@ -50,7 +57,7 @@ def tile_moe_shr_mlp_relu2_kernel(tc, xT, w1, w2, gate, offs, pos1, pos2, out):
                 nc.sync.dma_start(t[:], w1[int(name[3:])].rearrange("(p j) i -> p j i", j=4))
                 raw[name] = t
 
-        for name in ["w1_4","w1_3","w1_7","w1_6","w2_A","w1_8","w2_C","w1_5","w28","w1_0","w1_2","w1_1","w2_B","g"]:
+        for name in ("w1_8", "w1_7", "w1_6", ("w1_2", "w1_0"), "w1_1", ("w1_3", "w1_5"), "w1_4", "w2_B", "w2_A", "w28", "g"):
             load(name)
         warm = keep.tile([P, 8], F32, name="warm")
         nc.gpsimd.memset(warm[:], 0.0)
@@ -66,20 +73,27 @@ def tile_moe_shr_mlp_relu2_kernel(tc, xT, w1, w2, gate, offs, pos1, pos2, out):
                 nc.gpsimd.tensor_scalar(dst, src, 1.0, 0.0, ALU.mult, ALU.add)
 
         x_pair = keep.tile([P, 2, T, 2], BF16, name="x_pair", align_bytes=64)
-        XV = 320
+        XV = (384, 0)
 
         def cast(u):
             src = x_raw[u][:].rearrange("p j t -> p t j")
-            nc.vector.tensor_copy(x_pair[:, u, 0:XV, :], src[:, 0:XV, :])
-            if XV < T:
-                nc.scalar.copy(x_pair[:, u, XV:T, :], src[:, XV:T, :])
+            cut = (XV)[u]
+            if cut > 0:
+                nc.vector.tensor_copy(x_pair[:, u, 0:cut, :], src[:, 0:cut, :])
+            if cut < T:
+                nc.scalar.copy(x_pair[:, u, cut:T, :], src[:, cut:T, :])
 
         words = x_pair[:].rearrange("p u t j -> p (u t j)").bitcast(U32)
         gx = keep.tile([P, E * C, 2], U32, name="gx", align_bytes=64)
+        planes = keep.tile([P, 2, E * C], U32, name="planes", align_bytes=64)
 
         def gath(g, u):
             lo, hi = CUTS[g], CUTS[g + 1]
-            nc.vector.tensor_copy(gx[:, lo:hi, u], words[:, u * T : (u + 1) * T].indirect(offs_t[:, lo // 16 : hi // 16]))
+            nc.vector.tensor_copy(planes[:, u, lo:hi], words[:, u * T : (u + 1) * T].indirect(offs_t[:, lo // 16 : hi // 16]))
+
+        def gi(g):
+            lo, hi = CUTS[g], CUTS[g + 1]
+            nc.gpsimd.tensor_copy(gx[:, lo:hi, :], planes[:, :, lo:hi].rearrange("p u s -> p s u"))
 
         def quant(in_, width, name):
             codes = keep.tile([P, width], U32, name=name + "_q", align_bytes=64)
@@ -92,7 +106,10 @@ def tile_moe_shr_mlp_relu2_kernel(tc, xT, w1, w2, gate, offs, pos1, pos2, out):
 
         def xall(engine):
             t = keep.tile([P, T, 2, 2], BF16, name="x_all", align_bytes=64)
-            copy_on(engine, t[:], x_pair[:].rearrange("p u t j -> p t u j"))
+            if engine == "G":
+                nc.gpsimd.tensor_copy(t[:].rearrange("p t u j -> p (t u j)").bitcast(U32).rearrange("p (t u) -> p t u", u=2), words.rearrange("p (u t) -> p t u", u=2))
+            else:
+                copy_on(engine, t[:], x_pair[:].rearrange("p u t j -> p t u j"))
             bf["xs"] = t
 
         def qxs():
@@ -101,23 +118,33 @@ def tile_moe_shr_mlp_relu2_kernel(tc, xT, w1, w2, gate, offs, pos1, pos2, out):
         def lay(name, parts):
             if name in W2:
                 d = keep.tile([P, W2[name][1] * 4 * N], BF16, name=name + "_bf", align_bytes=64)
-                dst = d[:].rearrange("p (e n j) -> p e n j", n=N, j=4)
-                src = raw[name][:].rearrange("p e j n -> p e n j")
+                dst = d[:].rearrange("p (e c i j) -> p e c j i", c=N // 4, i=4, j=4)
+                src = raw[name][:].rearrange("p e j (c i) -> p e c j i", i=4)
             else:
-                d = keep.tile([P, 4 * H], BF16, name=name + "_bf", align_bytes=64)
-                dst = d[:].rearrange("p (t m j) -> p m j t", t=4, j=4)
+                group = GROUPS.get(name, (name,))
+                if group[0] not in bf_all:
+                    bf_all[group[0]] = keep.tile([P, len(group) * 4 * H], BF16, name=group[0] + "_bf", align_bytes=64)
+                at = group.index(name) * 4 * H
+                d = bf_all[group[0]][:, at : at + 4 * H]
+                dst = d.rearrange("p (t m j) -> p m j t", t=4, j=4)
                 src = raw[name][:].rearrange("p j (m t) -> p m j t", t=4)
             lo = 0
             for engine, hi in parts:
                 if name in W2:
-                    copy_on(engine, dst[:, :, lo:hi, :], src[:, :, lo:hi, :])
+                    copy_on(engine, dst[:, :, lo // 4 : hi // 4], src[:, :, lo // 4 : hi // 4])
                 else:
                     copy_on(engine, dst[:, lo:hi], src[:, lo:hi])
                 lo = hi
             bf[name] = d
 
         def q(name):
-            qz[name] = quant(bf[name][:], bf[name].shape[1] // 4, name)
+            if name in W2:
+                qz[name] = quant(bf[name][:], bf[name].shape[1] // 4, name)
+                return
+            group = GROUPS.get(name, (name,))
+            codes, scales = quant(bf_all[group[0]][:], len(group) * H, group[0])
+            for i, k in enumerate(group):
+                qz[k] = (codes[:, i * H : (i + 1) * H], scales[:, i * H : (i + 1) * H])
 
         def layer1(key, weights, tokens, c0):
             acc = ps.tile([P, 4, C], F32, name=f"acc{len(accs) % 5}")
@@ -172,118 +199,120 @@ def tile_moe_shr_mlp_relu2_kernel(tc, xT, w1, w2, gate, offs, pos1, pos2, out):
         ys = ps.tile([P, T], F32, name="ys")
         ot = keep.tile([P, T], F32, name="ot")
 
-        lay("w1_8", [("V", 96), ("S", 128)])
-        lay("w1_0", [("V", 128)])
-        lay("w1_3", [("V", 64), ("S", 128)])
-        lay("w1_7", [("S", 128)])
-        lay("w1_1", [("V", 96), ("S", 128)])
-        lay("w28", [("V", 80), ("S", 128)])
-        cast(1)
-        cast(0)
-        lay("w1_4", [("V", 48), ("S", 128)])
-        gath(0, 0)
-        q("w1_4")
-        gath(1, 0)
-        gath(1, 1)
+        lay("w1_0", [("V", 96), ("S", 128)])
+        lay("w1_3", [("V", 80), ("S", 128)])
+        lay("w28", [("V", 48), ("S", 128)])
+        lay("w1_4", [("V", 96), ("S", 128)])
+        lay("w1_8", [("S", 128)])
         q("w1_8")
-        q("w1_1")
-        gath(0, 1)
-        xall("S")
+        cast(0)
+        gath(1, 0)
+        cast(1)
+        gath(1, 1)
+        xall("G")
+        lay("w1_7", [("S", 128)])
         q("w1_7")
-        lay("w1_6", [("V", 48), ("S", 128)])
-        lay("w2_A", [("V", 64), ("S", 128)])
-        qx(0)
-        gath(2, 0)
-        lay("w2_B", [("V", 128)])
-        q("w2_B")
+        lay("w1_6", [("S", 128)])
         qxs()
-        lay("w1_2", [("V", 128)])
-        lay("w1_5", [("V", 80), ("S", 128)])
-        gath(2, 1)
-        q("w1_6")
-        q("w1_0")
-        q("w1_2")
-        mms(1)
-        qx(1)
-        q("w1_5")
         mms(0)
-        mm(5)
-        relu("s1", raw["w1_0"][:].rearrange("p j i -> p (j i)")[:, 0:1024][:, 512:1024])
-        mm(0)
-        q("w1_3")
-        mm(3)
-        q("w28")
-        relu("s0", raw["w1_0"][:].rearrange("p j i -> p (j i)")[:, 0:1024][:, 0:512])
-        mm(6)
-        mm(4)
-        r_3 = keep.tile([P, 1024], F32, name="r_3", align_bytes=64)
-        relu(6, r_3[:][:, 0:512])
-        relu(3, raw["w1_5"][:].rearrange("p j i -> p (j i)")[:, 0:1024][:, 512:1024])
-        relu(5, raw["w1_7"][:].rearrange("p j i -> p (j i)")[:, 0:1024][:, 512:1024])
-        relu(4, raw["w1_7"][:].rearrange("p j i -> p (j i)")[:, 0:1024][:, 0:512])
-        square("V", raw["w1_2"][:].rearrange("p j i -> p (j i)")[:, 0:512].bitcast(BF16), raw["w1_0"][:].rearrange("p j i -> p (j i)")[:, 0:1024])
-        mm(1)
-        relu(0, raw["w1_0"][:].rearrange("p j i -> p (j i)")[:, 1024:2048][:, 0:512])
-        mm(2)
-        mm(7)
-        relu(7, r_3[:][:, 512:1024])
-        mms(2)
-        square("S", raw["w1_1"][:].rearrange("p j i -> p (j i)")[:, 0:512].bitcast(BF16), raw["w1_7"][:].rearrange("p j i -> p (j i)")[:, 0:1024])
-        relu(1, raw["w1_0"][:].rearrange("p j i -> p (j i)")[:, 1024:2048][:, 512:1024])
-        lay("w2_C", [("S", 128)])
-        square("V", raw["w1_7"][:].rearrange("p j i -> p (j i)")[:, 1024:1536].bitcast(BF16), r_3[:])
-        relu("s2", raw["w1_5"][:].rearrange("p j i -> p (j i)")[:, 1024:2048][:, 0:512])
-        relu(2, raw["w1_5"][:].rearrange("p j i -> p (j i)")[:, 0:1024][:, 0:512])
-        square("S", raw["w1_1"][:].rearrange("p j i -> p (j i)")[:, 512:1024].bitcast(BF16), raw["w1_5"][:].rearrange("p j i -> p (j i)")[:, 0:1024])
-        hq_3 = keep.tile([P, 256], U32, name="hq_3", align_bytes=64)
-        hz_3 = keep.tile([P, 256], U8, name="hz_3", align_bytes=64)
-        qh(hq_3[:], hz_3[:], raw["w1_7"][:].rearrange("p j i -> p (j i)")[:, 1024:1536].bitcast(BF16))
         mms(3)
-        hq_1 = keep.tile([P, 256], U32, name="hq_1", align_bytes=64)
-        hz_1 = keep.tile([P, 256], U8, name="hz_1", align_bytes=64)
-        qh(hq_1[:], hz_1[:], raw["w1_1"][:].rearrange("p j i -> p (j i)")[:, 512:1024].bitcast(BF16))
-        q("w2_C")
-        yp[3] = ps.tile([P, 256], F32, name="yp0")
-        second("w2_C", 0, hq_3[:, 0:128], hz_3[:, 0:128], yp[3][:, 0:128])
-        second("w2_C", 128, hq_3[:, 128:256], hz_3[:, 128:256], yp[3][:, 128:256])
+        q("w1_0")
+        lay("w1_5", [("V", 96), ("S", 128)])
+        gi(1)
+        q("w1_5")
+        gath(2, 0)
+        lay("w1_1", [("V", 64), ("S", 128)])
+        q("w1_4")
+        lay("w2_B", [("V", 128)])
+        gath(0, 1)
+        q("w2_B")
+        mms(2)
+        q("w1_6")
+        gath(2, 1)
+        relu("s3", raw["w1_0"][:].rearrange("p j i -> p (j i)")[:, 0:1024][:, 512:1024])
+        gi(2)
+        gath(0, 0)
+        gi(0)
+        qx(0)
+        relu("s2", raw["w1_0"][:].rearrange("p j i -> p (j i)")[:, 0:1024][:, 0:512])
+        lay("w1_2", [("V", 96), ("S", 128)])
+        qx(1)
+        mm(6)
+        relu(6, raw["w1_2"][:].rearrange("p j i -> p (j i)")[:, 0:1024][:, 0:512])
+        mm(7)
+        lay("w2_A", [("V", 80), ("S", 128)])
+        q("w1_3")
+        q("w1_1")
+        q("w1_2")
+        q("w28")
         q("w2_A")
-        hq_2 = keep.tile([P, 256], U32, name="hq_2", align_bytes=64)
-        hz_2 = keep.tile([P, 256], U8, name="hz_2", align_bytes=64)
-        qh(hq_2[:], hz_2[:], raw["w1_1"][:].rearrange("p j i -> p (j i)")[:, 0:512].bitcast(BF16))
-        square("S", raw["w1_6"][:].rearrange("p j i -> p (j i)")[:, 0:512].bitcast(BF16), raw["w1_0"][:].rearrange("p j i -> p (j i)")[:, 1024:2048])
-        relu("s3", raw["w1_5"][:].rearrange("p j i -> p (j i)")[:, 1024:2048][:, 512:1024])
-        hq_0 = keep.tile([P, 256], U32, name="hq_0", align_bytes=64)
-        hz_0 = keep.tile([P, 256], U8, name="hz_0", align_bytes=64)
-        qh(hq_0[:], hz_0[:], raw["w1_6"][:].rearrange("p j i -> p (j i)")[:, 0:512].bitcast(BF16))
-        yp[1] = ps.tile([P, 256], F32, name="yp1")
-        second("w2_A", 256, hq_1[:, 0:128], hz_1[:, 0:128], yp[1][:, 0:128])
-        second("w2_A", 384, hq_1[:, 128:256], hz_1[:, 128:256], yp[1][:, 128:256])
-        nc.scalar.copy(yt[:, 768:1024], yp[3][:])
+        relu(7, raw["w1_2"][:].rearrange("p j i -> p (j i)")[:, 0:1024][:, 512:1024])
+        h_3 = keep.tile([P, 1024], BF16, name="h_3", align_bytes=64)
+        square("V", h_3[:][:, 0:1024], raw["w1_2"][:].rearrange("p j i -> p (j i)")[:, 0:1024])
+        hq_m3 = keep.tile([P, 256], U32, name="hq_m3", align_bytes=64)
+        hz_m3 = keep.tile([P, 256], U8, name="hz_m3", align_bytes=64)
+        qh(hq_m3[:], hz_m3[:], h_3[:])
+        hq_3, hz_3 = hq_m3[:, 0:256], hz_m3[:, 0:256]
+        relu("s0", raw["w1_6"][:].rearrange("p j i -> p (j i)")[:, 0:1024][:, 0:512])
+        mm(5)
+        relu(5, raw["w1_3"][:].rearrange("p j i -> p (j i)")[:, 0:1024][:, 512:1024])
+        mm(1)
+        relu(1, raw["w1_5"][:].rearrange("p j i -> p (j i)")[:, 0:1024][:, 512:1024])
+        mm(2)
+        relu(2, raw["w1_0"][:].rearrange("p j i -> p (j i)")[:, 1024:2048][:, 0:512])
+        mms(1)
+        relu("s1", raw["w1_6"][:].rearrange("p j i -> p (j i)")[:, 0:1024][:, 512:1024])
+        square("S", raw["w1_3"][:].rearrange("p j i -> p (j i)")[:, 1024:1536].bitcast(BF16), raw["w1_6"][:].rearrange("p j i -> p (j i)")[:, 0:1024])
+        mm(0)
+        relu(0, raw["w1_5"][:].rearrange("p j i -> p (j i)")[:, 0:1024][:, 0:512])
+        mm(4)
+        relu(4, raw["w1_3"][:].rearrange("p j i -> p (j i)")[:, 0:1024][:, 0:512], "V")
+        square("V", raw["w1_5"][:].rearrange("p j i -> p (j i)")[:, 1024:1536].bitcast(BF16), raw["w1_0"][:].rearrange("p j i -> p (j i)")[:, 0:1024])
+        square("S", raw["w1_1"][:].rearrange("p j i -> p (j i)")[:, 0:512].bitcast(BF16)[:, 0:1024], raw["w1_3"][:].rearrange("p j i -> p (j i)")[:, 0:1024])
+        hq_m2 = keep.tile([P, 256], U32, name="hq_m2", align_bytes=64)
+        hz_m2 = keep.tile([P, 256], U8, name="hz_m2", align_bytes=64)
+        qh(hq_m2[:], hz_m2[:], raw["w1_1"][:].rearrange("p j i -> p (j i)")[:, 0:512].bitcast(BF16))
+        hq_2, hz_2 = hq_m2[:, 0:256], hz_m2[:, 0:256]
         yp[2] = ps.tile([P, 256], F32, name="yp0")
         second("w2_B", 0, hq_2[:, 0:128], hz_2[:, 0:128], yp[2][:, 0:128])
         second("w2_B", 128, hq_2[:, 128:256], hz_2[:, 128:256], yp[2][:, 128:256])
-        nc.scalar.copy(yt[:, 256:512], yp[1][:])
         nc.scalar.copy(yt[:, 512:768], yp[2][:])
+        mm(3)
+        square("S", raw["w1_7"][:].rearrange("p j i -> p (j i)")[:, 0:1024].bitcast(BF16)[:, 0:1024], raw["w1_5"][:].rearrange("p j i -> p (j i)")[:, 0:1024])
+        relu(3, raw["w1_0"][:].rearrange("p j i -> p (j i)")[:, 1024:2048][:, 512:1024])
+        square("S", raw["w1_7"][:].rearrange("p j i -> p (j i)")[:, 0:1024].bitcast(BF16)[:, 1024:2048], raw["w1_0"][:].rearrange("p j i -> p (j i)")[:, 1024:2048])
+        hq_m0 = keep.tile([P, 512], U32, name="hq_m0", align_bytes=64)
+        hz_m0 = keep.tile([P, 512], U8, name="hz_m0", align_bytes=64)
+        qh(hq_m0[:], hz_m0[:], raw["w1_7"][:].rearrange("p j i -> p (j i)")[:, 0:1024].bitcast(BF16))
+        hq_0, hz_0 = hq_m0[:, 0:256], hz_m0[:, 0:256]
+        hq_1, hz_1 = hq_m0[:, 256:512], hz_m0[:, 256:512]
         yp[0] = ps.tile([P, 256], F32, name="yp1")
         second("w2_A", 0, hq_0[:, 0:128], hz_0[:, 0:128], yp[0][:, 0:128])
         second("w2_A", 128, hq_0[:, 128:256], hz_0[:, 128:256], yp[0][:, 128:256])
         nc.scalar.copy(yt[:, 0:256], yp[0][:])
-        square("V", raw["w1_7"][:].rearrange("p j i -> p (j i)")[:, 1536:2048].bitcast(BF16), raw["w1_5"][:].rearrange("p j i -> p (j i)")[:, 1024:2048])
-        part_0 = keep.tile([P, T], F32, name="part_0")
-        nc.vector.tensor_tensor(part_0[:], yt[:].indirect(misc["pos"][0][:]), misc["g"][:, 0, :], ALU.mult)
-        part_1 = keep.tile([P, T], F32, name="part_1")
-        nc.vector.tensor_tensor(part_1[:], yt[:].indirect(misc["pos"][1][:]), misc["g"][:, 1, :], ALU.mult)
         hq_s1 = keep.tile([P, 256], U32, name="hq_s1", align_bytes=64)
         hz_s1 = keep.tile([P, 256], U8, name="hz_s1", align_bytes=64)
-        qh(hq_s1[:], hz_s1[:], raw["w1_7"][:].rearrange("p j i -> p (j i)")[:, 1536:2048].bitcast(BF16))
+        qh(hq_s1[:], hz_s1[:], raw["w1_5"][:].rearrange("p j i -> p (j i)")[:, 1024:1536].bitcast(BF16))
+        second("w28", 0, hq_s1[:], hz_s1[:], ys[:, 256:512])
         hq_s0 = keep.tile([P, 256], U32, name="hq_s0", align_bytes=64)
         hz_s0 = keep.tile([P, 256], U8, name="hz_s0", align_bytes=64)
-        qh(hq_s0[:], hz_s0[:], raw["w1_2"][:].rearrange("p j i -> p (j i)")[:, 0:512].bitcast(BF16))
+        qh(hq_s0[:], hz_s0[:], raw["w1_3"][:].rearrange("p j i -> p (j i)")[:, 1024:1536].bitcast(BF16))
         second("w28", 0, hq_s0[:], hz_s0[:], ys[:, 0:256])
-        second("w28", 0, hq_s1[:], hz_s1[:], ys[:, 256:512])
+        yp[1] = ps.tile([P, 256], F32, name="yp0")
+        second("w2_A", 256, hq_1[:, 0:128], hz_1[:, 0:128], yp[1][:, 0:128])
+        second("w2_A", 384, hq_1[:, 128:256], hz_1[:, 128:256], yp[1][:, 128:256])
+        yp[3] = ps.tile([P, 256], F32, name="yp1")
+        second("w2_B", 256, hq_3[:, 0:128], hz_3[:, 0:128], yp[3][:, 0:128])
+        second("w2_B", 384, hq_3[:, 128:256], hz_3[:, 128:256], yp[3][:, 128:256])
+        nc.scalar.copy(yt[:, 768:1024], yp[3][:])
+        nc.scalar.copy(yt[:, 256:512], yp[1][:])
+        part_1 = keep.tile([P, T], F32, name="part_1")
+        nc.vector.tensor_tensor(part_1[:], yt[:].indirect(misc["pos"][1][:]), misc["g"][:, 1, :], ALU.mult)
+        part_0 = keep.tile([P, T], F32, name="part_0")
+        nc.vector.tensor_tensor(part_0[:], yt[:].indirect(misc["pos"][0][:]), misc["g"][:, 0, :], ALU.mult)
         both = keep.tile([P, T], F32, name="both")
         nc.vector.tensor_tensor(both[:], part_0[:], part_1[:], ALU.add)
-        nc.vector.tensor_tensor(ot[:, 256:512], ys[:, 256:512], both[:, 256:512], ALU.add)
-        nc.sync.dma_start(out[:, 256:512], ot[:, 256:512])
         nc.vector.tensor_tensor(ot[:, 0:256], ys[:, 0:256], both[:, 0:256], ALU.add)
         nc.sync.dma_start(out[:, 0:256], ot[:, 0:256])
+        nc.vector.tensor_tensor(ot[:, 256:512], ys[:, 256:512], both[:, 256:512], ALU.add)
+        nc.sync.dma_start(out[:, 256:512], ot[:, 256:512])

import concourse.mybir as mybir

E, C, T, K, H, N = 8, 128, 512, 512, 512, 128
P = 128
FLOPS = 2 * K * H * (E * C + T) + 2 * H * N * (E * C + T)
F32 = mybir.dt.float32
BF16 = mybir.dt.bfloat16
U32 = mybir.dt.uint32
U16 = mybir.dt.uint16
U8 = mybir.dt.uint8
FP8X4 = mybir.dt.float8_e4m3fn_x4
ACT = mybir.ActivationFunctionType
ALU = mybir.AluOpType
CUTS = (0, 384, 768, 1024)
GROUPS = {}
W2 = {"w2_A": (0, 4), "w2_B": (4, 4), "w28": (8, 1)}


def tile_moe_shr_mlp_relu2_kernel(tc, xT, w1, w2, gate, offs, pos1, pos2, out):
    nc = tc.nc
    with (
        tc.tile_pool(name="keep", bufs=1) as keep,
        tc.psum_pool(name="ps", bufs=1) as ps,
    ):
        offs_t = keep.tile([P, E * C // 16], U16, name="offs_t")
        nc.sync.dma_start(offs_t[:], offs)
        bf_all = {}
        x_raw, raw, bf, qz, accs, misc, yp = [], {}, {}, {}, {}, {}, {}
        xv = xT.rearrange("(p j) t -> p j t", j=4)
        for u in range(2):
            xr = keep.tile([P, 2, T], F32, name=f"x_raw{u}")
            (nc.sync if u else nc.scalar).dma_start(xr[:], xv[:, 2 * u : 2 * u + 2, :])
            x_raw.append(xr)

        def load(name):
            if isinstance(name, tuple):
                a, b = sorted(int(k[3:]) for k in name)
                t = keep.tile([P, 2, 4, H], F32, name=f"w1_raw{a}_{b}")
                nc.sync.dma_start(t[:], w1[a : b + 1 : b - a].rearrange("e (p j) i -> p e j i", j=4))
                raw[f"w1_{a}"], raw[f"w1_{b}"] = t[:, 0], t[:, 1]
            elif name == "g":
                pos = []
                for i, src in enumerate((pos1, pos2)):
                    t = keep.tile([P, T // 16], U16, name=f"pos{i}")
                    nc.sync.dma_start(t[:], src)
                    pos.append(t)
                g = keep.tile([P, 2, T], F32, name="gates")
                nc.sync.dma_start(g[:], gate.rearrange("r p t -> p r t"))
                misc["g"], misc["pos"] = g, pos
            elif name in W2:
                e0, n = W2[name]
                t = keep.tile([P, n, 4, N], F32, name=name + "_raw")
                nc.sync.dma_start(t[:], w2[e0 : e0 + n].rearrange("e (p j) n -> p e j n", j=4))
                raw[name] = t
            else:
                t = keep.tile([P, 4, H], F32, name=name + "_raw")
                nc.sync.dma_start(t[:], w1[int(name[3:])].rearrange("(p j) i -> p j i", j=4))
                raw[name] = t

        for name in ("w1_8", "w1_7", "w1_6", ("w1_2", "w1_0"), "w1_1", ("w1_3", "w1_5"), "w1_4", "w2_B", "w2_A", "w28", "g"):
            load(name)
        warm = keep.tile([P, 8], F32, name="warm")
        nc.gpsimd.memset(warm[:], 0.0)
        warm_out = keep.tile([P, 8], F32, name="warm_out")
        nc.scalar.activation(warm_out[:], warm[:], ACT.Square)

        def copy_on(engine, dst, src):
            if engine == "V":
                nc.vector.tensor_copy(dst, src)
            elif engine == "S":
                nc.scalar.copy(dst, src)
            else:
                nc.gpsimd.tensor_scalar(dst, src, 1.0, 0.0, ALU.mult, ALU.add)

        x_pair = keep.tile([P, 2, T, 2], BF16, name="x_pair", align_bytes=64)
        XV = (384, 0)

        def cast(u):
            src = x_raw[u][:].rearrange("p j t -> p t j")
            cut = (XV)[u]
            if cut > 0:
                nc.vector.tensor_copy(x_pair[:, u, 0:cut, :], src[:, 0:cut, :])
            if cut < T:
                nc.scalar.copy(x_pair[:, u, cut:T, :], src[:, cut:T, :])

        words = x_pair[:].rearrange("p u t j -> p (u t j)").bitcast(U32)
        gx = keep.tile([P, E * C, 2], U32, name="gx", align_bytes=64)
        planes = keep.tile([P, 2, E * C], U32, name="planes", align_bytes=64)

        def gath(g, u):
            lo, hi = CUTS[g], CUTS[g + 1]
            nc.vector.tensor_copy(planes[:, u, lo:hi], words[:, u * T : (u + 1) * T].indirect(offs_t[:, lo // 16 : hi // 16]))

        def gi(g):
            lo, hi = CUTS[g], CUTS[g + 1]
            nc.gpsimd.tensor_copy(gx[:, lo:hi, :], planes[:, :, lo:hi].rearrange("p u s -> p s u"))

        def quant(in_, width, name):
            codes = keep.tile([P, width], U32, name=name + "_q", align_bytes=64)
            scales = keep.tile([P, width], U8, name=name + "_s", align_bytes=64)
            nc.vector.quantize_mx(out=codes[:].bitcast(FP8X4), scales=scales[:], in_=in_)
            return codes, scales

        def qx(h):
            qz[f"x{h}"] = quant(gx[:, h * 512 : (h + 1) * 512, :].rearrange("p s u -> p (s u)").bitcast(BF16), 512, f"gx{h}")

        def xall(engine):
            t = keep.tile([P, T, 2, 2], BF16, name="x_all", align_bytes=64)
            if engine == "G":
                nc.gpsimd.tensor_copy(t[:].rearrange("p t u j -> p (t u j)").bitcast(U32).rearrange("p (t u) -> p t u", u=2), words.rearrange("p (u t) -> p t u", u=2))
            else:
                copy_on(engine, t[:], x_pair[:].rearrange("p u t j -> p t u j"))
            bf["xs"] = t

        def qxs():
            qz["xs"] = quant(bf["xs"][:].rearrange("p t u j -> p (t u j)"), T, "xs")

        def lay(name, parts):
            if name in W2:
                d = keep.tile([P, W2[name][1] * 4 * N], BF16, name=name + "_bf", align_bytes=64)
                dst = d[:].rearrange("p (e c i j) -> p e c j i", c=N // 4, i=4, j=4)
                src = raw[name][:].rearrange("p e j (c i) -> p e c j i", i=4)
            else:
                group = GROUPS.get(name, (name,))
                if group[0] not in bf_all:
                    bf_all[group[0]] = keep.tile([P, len(group) * 4 * H], BF16, name=group[0] + "_bf", align_bytes=64)
                at = group.index(name) * 4 * H
                d = bf_all[group[0]][:, at : at + 4 * H]
                dst = d.rearrange("p (t m j) -> p m j t", t=4, j=4)
                src = raw[name][:].rearrange("p j (m t) -> p m j t", t=4)
            lo = 0
            for engine, hi in parts:
                if name in W2:
                    copy_on(engine, dst[:, :, lo // 4 : hi // 4], src[:, :, lo // 4 : hi // 4])
                else:
                    copy_on(engine, dst[:, lo:hi], src[:, lo:hi])
                lo = hi
            bf[name] = d

        def q(name):
            if name in W2:
                qz[name] = quant(bf[name][:], bf[name].shape[1] // 4, name)
                return
            group = GROUPS.get(name, (name,))
            codes, scales = quant(bf_all[group[0]][:], len(group) * H, group[0])
            for i, k in enumerate(group):
                qz[k] = (codes[:, i * H : (i + 1) * H], scales[:, i * H : (i + 1) * H])

        def layer1(key, weights, tokens, c0):
            acc = ps.tile([P, 4, C], F32, name=f"acc{len(accs) % 5}")
            for t in range(4):
                cols = slice(t * P, (t + 1) * P)
                nc.tensor.matmul_mx(
                    out=acc[:, t, :],
                    lhsT=weights[0][:, cols].bitcast(FP8X4),
                    lhsT_scale=weights[1][:, cols],
                    rhs=tokens[0][:, c0 : c0 + C].bitcast(FP8X4),
                    rhs_scale=tokens[1][:, c0 : c0 + C],
                    start=True,
                    stop=True,
                )
            accs[key] = acc

        def mm(e):
            layer1(e, qz[f"w1_{e}"], qz[f"x{e // 4}"], e % 4 * C)

        def mms(g):
            layer1(f"s{g}", qz["w1_8"], qz["xs"], g * C)

        def relu(key, r, engine="S"):
            dst, src = r.rearrange("p (c t) -> p c t", t=4), accs[key][:].rearrange("p t c -> p c t")
            if engine == "V":
                nc.vector.tensor_scalar_max(dst, src, 0.0)
            else:
                nc.scalar.activation(dst, src, ACT.Relu)

        def square(engine, h, r):
            if engine == "V":
                nc.vector.tensor_tensor(h, r, r, ALU.mult)
            else:
                nc.scalar.activation(h, r, ACT.Square)

        def qh(codes, scales, h):
            nc.vector.quantize_mx(out=codes.bitcast(FP8X4), scales=scales, in_=h)

        def second(name, c0, codes, scales, dst):
            weights = qz[name]
            nc.tensor.matmul_mx(
                out=dst,
                lhsT=weights[0][:, c0 : c0 + N].bitcast(FP8X4),
                lhsT_scale=weights[1][:, c0 : c0 + N],
                rhs=codes.bitcast(FP8X4),
                rhs_scale=scales,
                start=True,
                stop=True,
            )

        yt = keep.tile([P, E * C], F32, name="yt")
        ys = ps.tile([P, T], F32, name="ys")
        ot = keep.tile([P, T], F32, name="ot")

        lay("w1_0", [("V", 96), ("S", 128)])
        lay("w1_3", [("V", 80), ("S", 128)])
        lay("w28", [("V", 48), ("S", 128)])
        lay("w1_4", [("V", 96), ("S", 128)])
        lay("w1_8", [("S", 128)])
        q("w1_8")
        cast(0)
        gath(1, 0)
        cast(1)
        gath(1, 1)
        xall("G")
        lay("w1_7", [("S", 128)])
        q("w1_7")
        lay("w1_6", [("S", 128)])
        qxs()
        mms(0)
        mms(3)
        q("w1_0")
        lay("w1_5", [("V", 96), ("S", 128)])
        gi(1)
        q("w1_5")
        gath(2, 0)
        lay("w1_1", [("V", 64), ("S", 128)])
        q("w1_4")
        lay("w2_B", [("V", 128)])
        gath(0, 1)
        q("w2_B")
        mms(2)
        q("w1_6")
        gath(2, 1)
        relu("s3", raw["w1_0"][:].rearrange("p j i -> p (j i)")[:, 0:1024][:, 512:1024])
        gi(2)
        gath(0, 0)
        gi(0)
        qx(0)
        relu("s2", raw["w1_0"][:].rearrange("p j i -> p (j i)")[:, 0:1024][:, 0:512])
        lay("w1_2", [("V", 96), ("S", 128)])
        qx(1)
        mm(6)
        relu(6, raw["w1_2"][:].rearrange("p j i -> p (j i)")[:, 0:1024][:, 0:512])
        mm(7)
        lay("w2_A", [("V", 80), ("S", 128)])
        q("w1_3")
        q("w1_1")
        q("w1_2")
        q("w28")
        q("w2_A")
        relu(7, raw["w1_2"][:].rearrange("p j i -> p (j i)")[:, 0:1024][:, 512:1024])
        h_3 = keep.tile([P, 1024], BF16, name="h_3", align_bytes=64)
        square("V", h_3[:][:, 0:1024], raw["w1_2"][:].rearrange("p j i -> p (j i)")[:, 0:1024])
        hq_m3 = keep.tile([P, 256], U32, name="hq_m3", align_bytes=64)
        hz_m3 = keep.tile([P, 256], U8, name="hz_m3", align_bytes=64)
        qh(hq_m3[:], hz_m3[:], h_3[:])
        hq_3, hz_3 = hq_m3[:, 0:256], hz_m3[:, 0:256]
        relu("s0", raw["w1_6"][:].rearrange("p j i -> p (j i)")[:, 0:1024][:, 0:512])
        mm(5)
        relu(5, raw["w1_3"][:].rearrange("p j i -> p (j i)")[:, 0:1024][:, 512:1024])
        mm(1)
        relu(1, raw["w1_5"][:].rearrange("p j i -> p (j i)")[:, 0:1024][:, 512:1024])
        mm(2)
        relu(2, raw["w1_0"][:].rearrange("p j i -> p (j i)")[:, 1024:2048][:, 0:512])
        mms(1)
        relu("s1", raw["w1_6"][:].rearrange("p j i -> p (j i)")[:, 0:1024][:, 512:1024])
        square("S", raw["w1_3"][:].rearrange("p j i -> p (j i)")[:, 1024:1536].bitcast(BF16), raw["w1_6"][:].rearrange("p j i -> p (j i)")[:, 0:1024])
        mm(0)
        relu(0, raw["w1_5"][:].rearrange("p j i -> p (j i)")[:, 0:1024][:, 0:512])
        mm(4)
        relu(4, raw["w1_3"][:].rearrange("p j i -> p (j i)")[:, 0:1024][:, 0:512], "V")
        square("V", raw["w1_5"][:].rearrange("p j i -> p (j i)")[:, 1024:1536].bitcast(BF16), raw["w1_0"][:].rearrange("p j i -> p (j i)")[:, 0:1024])
        square("S", raw["w1_1"][:].rearrange("p j i -> p (j i)")[:, 0:512].bitcast(BF16)[:, 0:1024], raw["w1_3"][:].rearrange("p j i -> p (j i)")[:, 0:1024])
        hq_m2 = keep.tile([P, 256], U32, name="hq_m2", align_bytes=64)
        hz_m2 = keep.tile([P, 256], U8, name="hz_m2", align_bytes=64)
        qh(hq_m2[:], hz_m2[:], raw["w1_1"][:].rearrange("p j i -> p (j i)")[:, 0:512].bitcast(BF16))
        hq_2, hz_2 = hq_m2[:, 0:256], hz_m2[:, 0:256]
        yp[2] = ps.tile([P, 256], F32, name="yp0")
        second("w2_B", 0, hq_2[:, 0:128], hz_2[:, 0:128], yp[2][:, 0:128])
        second("w2_B", 128, hq_2[:, 128:256], hz_2[:, 128:256], yp[2][:, 128:256])
        nc.scalar.copy(yt[:, 512:768], yp[2][:])
        mm(3)
        square("S", raw["w1_7"][:].rearrange("p j i -> p (j i)")[:, 0:1024].bitcast(BF16)[:, 0:1024], raw["w1_5"][:].rearrange("p j i -> p (j i)")[:, 0:1024])
        relu(3, raw["w1_0"][:].rearrange("p j i -> p (j i)")[:, 1024:2048][:, 512:1024])
        square("S", raw["w1_7"][:].rearrange("p j i -> p (j i)")[:, 0:1024].bitcast(BF16)[:, 1024:2048], raw["w1_0"][:].rearrange("p j i -> p (j i)")[:, 1024:2048])
        hq_m0 = keep.tile([P, 512], U32, name="hq_m0", align_bytes=64)
        hz_m0 = keep.tile([P, 512], U8, name="hz_m0", align_bytes=64)
        qh(hq_m0[:], hz_m0[:], raw["w1_7"][:].rearrange("p j i -> p (j i)")[:, 0:1024].bitcast(BF16))
        hq_0, hz_0 = hq_m0[:, 0:256], hz_m0[:, 0:256]
        hq_1, hz_1 = hq_m0[:, 256:512], hz_m0[:, 256:512]
        yp[0] = ps.tile([P, 256], F32, name="yp1")
        second("w2_A", 0, hq_0[:, 0:128], hz_0[:, 0:128], yp[0][:, 0:128])
        second("w2_A", 128, hq_0[:, 128:256], hz_0[:, 128:256], yp[0][:, 128:256])
        nc.scalar.copy(yt[:, 0:256], yp[0][:])
        hq_s1 = keep.tile([P, 256], U32, name="hq_s1", align_bytes=64)
        hz_s1 = keep.tile([P, 256], U8, name="hz_s1", align_bytes=64)
        qh(hq_s1[:], hz_s1[:], raw["w1_5"][:].rearrange("p j i -> p (j i)")[:, 1024:1536].bitcast(BF16))
        second("w28", 0, hq_s1[:], hz_s1[:], ys[:, 256:512])
        hq_s0 = keep.tile([P, 256], U32, name="hq_s0", align_bytes=64)
        hz_s0 = keep.tile([P, 256], U8, name="hz_s0", align_bytes=64)
        qh(hq_s0[:], hz_s0[:], raw["w1_3"][:].rearrange("p j i -> p (j i)")[:, 1024:1536].bitcast(BF16))
        second("w28", 0, hq_s0[:], hz_s0[:], ys[:, 0:256])
        yp[1] = ps.tile([P, 256], F32, name="yp0")
        second("w2_A", 256, hq_1[:, 0:128], hz_1[:, 0:128], yp[1][:, 0:128])
        second("w2_A", 384, hq_1[:, 128:256], hz_1[:, 128:256], yp[1][:, 128:256])
        yp[3] = ps.tile([P, 256], F32, name="yp1")
        second("w2_B", 256, hq_3[:, 0:128], hz_3[:, 0:128], yp[3][:, 0:128])
        second("w2_B", 384, hq_3[:, 128:256], hz_3[:, 128:256], yp[3][:, 128:256])
        nc.scalar.copy(yt[:, 768:1024], yp[3][:])
        nc.scalar.copy(yt[:, 256:512], yp[1][:])
        part_1 = keep.tile([P, T], F32, name="part_1")
        nc.vector.tensor_tensor(part_1[:], yt[:].indirect(misc["pos"][1][:]), misc["g"][:, 1, :], ALU.mult)
        part_0 = keep.tile([P, T], F32, name="part_0")
        nc.vector.tensor_tensor(part_0[:], yt[:].indirect(misc["pos"][0][:]), misc["g"][:, 0, :], ALU.mult)
        both = keep.tile([P, T], F32, name="both")
        nc.vector.tensor_tensor(both[:], part_0[:], part_1[:], ALU.add)
        nc.vector.tensor_tensor(ot[:, 0:256], ys[:, 0:256], both[:, 0:256], ALU.add)
        nc.sync.dma_start(out[:, 0:256], ot[:, 0:256])
        nc.vector.tensor_tensor(ot[:, 256:512], ys[:, 256:512], both[:, 256:512], ALU.add)
        nc.sync.dma_start(out[:, 256:512], ot[:, 256:512])
